import numpy as np
import ml_dtypes


def mxq(x, axis, fmt="e4m3"):
    dtype, down = {"e4m3": (ml_dtypes.float8_e4m3fn, 7), "e5m2": (ml_dtypes.float8_e5m2, 14)}[fmt]
    v = np.moveaxis(np.asarray(x, np.float32).astype(ml_dtypes.bfloat16).astype(np.float64), axis, -1)
    blocks = v.reshape(v.shape[:-1] + (-1, 32))
    amax = np.abs(blocks).max(-1, keepdims=True)
    byte = np.maximum(np.where(amax > 0, np.frexp(amax)[1] - 1 + 127, 0) - down, 1)
    scale = np.exp2(byte - 127.0)
    codes = (blocks / scale).astype(np.float32).astype(dtype).astype(np.float64)
    return np.moveaxis((codes * scale).reshape(v.shape), -1, axis)


WIDE = False


def mx_kscale(k):
    if not WIDE:
        return np.ones(k)
    levels = np.array([10, -10, 5, -5, 0])
    if k % 512:
        return np.exp2(np.random.permutation(np.resize(levels, k // 32))).repeat(32)
    a = np.empty((k // 512, 16))
    for p in range(k // 512):
        a[p, :8] = np.random.permutation(np.resize(levels, 8))
        for g in range(8):
            far = levels[np.abs(levels - a[p, g]) >= 10]
            a[p, g + 8] = far[np.random.randint(len(far))]
    return np.exp2(a.ravel()).repeat(32)


BF16 = ml_dtypes.bfloat16


def bf(x):
    return np.asarray(x, np.float32).astype(BF16)


def f64(x):
    return np.asarray(x).astype(np.float64)


E2M1 = np.array([0.0, 0.5, 1.0, 1.5, 2.0, 3.0, 4.0, 6.0, -0.0, -0.5, -1.0, -1.5, -2.0, -3.0, -4.0, -6.0])


def pack_weight(w, fmt):
    k, n = w.shape
    w = f64(bf(w)).reshape(k // 32, 32, n)
    amax = np.abs(w).max(1)
    if fmt == "e4m3":
        byte = np.frexp(amax)[1] - 1 + 127 - 7
    else:
        mant, ex = np.frexp(amax / 6.0)
        byte = np.where(mant > 0.5, ex, ex - 1) + 127
    byte = np.clip(np.where(amax > 0, byte, 1), 1, 254)
    scaled = (w * np.exp2(127.0 - byte)[:, None, :]).reshape(k, n).astype(np.float32)
    by_word = np.ascontiguousarray(scaled.reshape(k // 512, 128, 4, n).transpose(0, 1, 3, 2))
    if fmt == "e4m3":
        words = by_word.astype(ml_dtypes.float8_e4m3fn).view(np.uint8)
    else:
        c = by_word.astype(ml_dtypes.float4_e2m1fn).view(np.uint8) & 0xF
        words = c[..., 0::2] | (c[..., 1::2] << 4)
    return np.ascontiguousarray(words), np.ascontiguousarray(byte.astype(np.uint8).reshape(k // 512, 16, n))


def unpack_weight(words, scales, fmt):
    g, p, n, _ = words.shape
    if fmt == "e4m3":
        vals = np.ascontiguousarray(words).view(ml_dtypes.float8_e4m3fn).astype(np.float64)
    else:
        nib = np.empty((g, p, n, 4), np.uint8)
        nib[..., 0::2] = words & 0xF
        nib[..., 1::2] = words >> 4
        vals = E2M1[nib]
    vals = vals * np.repeat(np.exp2(scales.astype(np.float64) - 127.0), 8, axis=1)[..., None]
    return vals.transpose(0, 1, 3, 2).reshape(g * 512, n)
def pack4(w):
    words, scales = pack_weight(w, "e2m1")
    return words.reshape(words.shape[0], 128, -1), scales


def unpack4(words, scales):
    return unpack_weight(words.reshape(words.shape[0], 128, -1, 2), scales, "e2m1")


def planes(Y):
    n, m = Y.shape
    b = f64(bf(Y)).reshape(n // 32, 32, m)
    amax = np.abs(b).max(1)
    byte = np.clip(np.where(amax > 0, np.frexp(amax)[1] - 1 + 127 - 7, 1), 1, 254)
    codes = (b * np.exp2(127.0 - byte)[:, None, :]).reshape(n, m).astype(np.float32).astype(ml_dtypes.float8_e4m3fn).view(np.uint8)
    words = codes.reshape(n // 512, 128, 4, m).transpose(0, 1, 3, 2)
    return np.ascontiguousarray(words), np.ascontiguousarray(byte.astype(np.uint8).reshape(n // 512, 16, m))


R, S, K1, K2 = 2048, 1024, 512, 1536
BOUND_MEAN, BOUND_STD, WEIGHT_SPREAD = -2.0, 0.5, 0.7

def setup_inputs():
    s1 = mx_kscale(K1)
    s2 = mx_kscale(K2)
    at = np.random.randn(K1, R) / np.sqrt(K1)
    x = np.random.randn(K1, S)
    wt = np.random.randn(K2, R) / np.sqrt(K2)
    u = np.random.randn(K2, S)
    wt_words, wt_scales = pack4(wt / s2[:, None])
    h = BOUND_MEAN + BOUND_STD * np.random.randn(R, S)
    rho = np.exp(WEIGHT_SPREAD * np.random.randn(R))
    return {
        "at": bf(at / s1[:, None]),
        "x": bf(x * s1[:, None]),
        "wt_words": wt_words,
        "wt_scales": wt_scales,
        "u": bf(u * s2[:, None]),
        "h": bf(h),
        "rho": bf(rho),
    }

def reference(at, x, wt_words, wt_scales, u, h, rho):
    first = mxq(f64(at), 0, "e4m3").T @ mxq(f64(x), 0, "e4m3")
    second = unpack4(wt_words, wt_scales).T @ mxq(f64(u), 0, "e4m3")
    y = f64(rho)[:, None] * np.maximum(first + second - f64(h), 0.0)
    words, scales = planes(y)
    return y, words, scales

@@ -1,0 +1,202 @@
+from contextlib import ExitStack
+
+import concourse.mybir as mybir
+
+R, S, K1, K2 = 2048, 1024, 512, 1536
+FLOPS = 2 * R * S * (K1 + K2)
+
+F32 = mybir.dt.float32
+BF16 = mybir.dt.bfloat16
+I32 = mybir.dt.int32
+U32 = mybir.dt.uint32
+U8 = mybir.dt.uint8
+FP8X4 = mybir.dt.float8_e4m3fn_x4
+FP4X4 = mybir.dt.float4_e2m1fn_x4
+ALU = mybir.AluOpType
+
+P = 128
+N = 512
+UNITS = [[0,0],[1,0],[2,0],[3,0],[0,1],[1,1],[2,1],[3,1]]
+Q_SYNC = "Lat0 Lw0 Lb00 Lsc0 Lsc1 Lsc2 Lsc3 Lb10 Lw1 Lb20 Lb30 Lw2 Lat1 Lh0 Lat23 Lh1 Lb01 Lb11 Lh2 Lb21 Lb31 Lh3 Sy0 Sy1 Sy2 Sy3 Sc0 Sc1 Sy4 Sc2 Sc3 Sy5 Sc4 Sy6 Sc5 Sy70 Sy71 Sy72 Sc6 Sy73 Sc7 Ss0 Ss1".split()
+Q_ACT = "Lrho ib00 ib10 ib20 ib30 ia1 ia2 ia3 ib01 ib11 ib21 ib31 io0 io1 io2 io3 io4 io5 io6 io7R Ss2 Ss3".split()
+Q_DVE = "zs ia0 qa0 wp00 wp01 wp02 wp03 qb00 sp0 sp1 sp2 sp3 qb10 wp10 wp11 qb20 wp12 wp13 wp20 wp21 qb30 wp22 s00 s01 r00 qa1 s02 r01 wp23 s03 r02 r03 s10 s11 r10 qa2 s12 r11 s13 r12 qa3 r13 s20 s21 r20 qb01 s22 r21 s23 r22 qb11 r23 s30 s31 r30 qb21 s32 r31 s33 r32 qb31 r33 s40 s41 r40 qo0 s42 r41 qo1 s43 r42 r43 qo2 s50 s51 r50 qo3 s52 r51 s53 r52 qo4 r53 s60 s61 r60 s62 r61 s63 r62 qo5 r63 s70 s71 r70 s72 r71 qo6 s73 r72 r73 io7L qo7L qo7R".split()
+Q_POOL = "".split()
+Q_PE = "m000 m010 m020 m030 m001 m011 m021 m031 m002 m012 m022 m032 m003 m013 m023 m033 m100 m101 m102 m103 m110 m111 m112 m113 m120 m121 m122 m123 m130 m131 m132 m133 m200 m201 m202 m203 m210 m211 m212 m213 m220 m221 m222 m223 m230 m231 m232 m233 m300 m301 m302 m303 m310 m311 m312 m313 m320 m321 m322 m323 m330 m331 m332 m333 m400 m401 m402 m403 m410 m411 m412 m413 m420 m421 m422 m423 m430 m431 m432 m433 m500 m501 m502 m503 m510 m511 m512 m513 m520 m521 m522 m523 m530 m531 m532 m533 m600 m601 m602 m603 m610 m611 m612 m613 m620 m621 m622 m623 m630 m631 m632 m633 m700 m701 m702 m703 m710 m711 m712 m713 m720 m721 m722 m723 m730 m731 m732 m733".split()
+
+
+def tile_two_stage_penalty_violation_g5_kernel(tc, at, x, wt_words, wt_scales, u, h, rho, out_0, out_1, out_2):
+    nc = tc.nc
+    with ExitStack() as ctx:
+        keep = ctx.enter_context(tc.tile_pool(name="keep", bufs=1))
+        stage = ctx.enter_context(tc.tile_pool(name="stage", bufs=4))
+        ypool = ctx.enter_context(tc.tile_pool(name="ypool", bufs=6))
+        cpool = ctx.enter_context(tc.tile_pool(name="cpool", bufs=4))
+        psum = ctx.enter_context(tc.psum_pool(name="psum", bufs=8))
+
+        at_raw = keep.tile([P, 4, R], BF16, align_bytes=64)
+        b_raw = keep.tile([P, 4, 4, S], BF16, align_bytes=64)
+        h_sb = keep.tile([P, 4, 4, S], BF16, align_bytes=64)
+        w_raw = keep.tile([P, 3, 2 * R], U8, align_bytes=64)
+        ws_raw = keep.tile([P, 3, R], U8, align_bytes=64)
+        w_codes = keep.tile([P, 4, 3, 2 * N], U8, align_bytes=64)
+        w_scales = keep.tile([P, 4, 3, N], U8, align_bytes=64)
+        a_codes = keep.tile([P, 4, N], U32, align_bytes=64)
+        a_scales = keep.tile([P, 4, N], U8, align_bytes=64)
+        b_codes = keep.tile([P, 4, S], U32, align_bytes=64)
+        b_scales = keep.tile([P, 4, S], U8, align_bytes=64)
+        y_scales = keep.tile([P, S], U8, align_bytes=64)
+        rho_sb = keep.tile([P, 4, 4], BF16, align_bytes=64)
+
+        grouped = {}
+        acc = {}
+        ytile = {}
+        ycodes = {}
+        steps = {}
+
+        def cols(i, w=N):
+            return slice(i * w, (i + 1) * w)
+
+        def b_src(ps):
+            src = x if ps == 0 else u[cols(ps - 1), :]
+            return src.rearrange("(p j) s -> p j s", j=4)
+
+        def add(name, deps, fn):
+            steps[name] = (deps, fn)
+
+        at_v = at.rearrange("(p j) r -> p j r", j=4)
+        for name, c0, c1 in [("0", 0, 1), ("1", 1, 2), ("2", 2, 3), ("3", 3, 4), ("01", 0, 2), ("23", 2, 4)]:
+            add("Lat" + name, [], lambda e, c0=c0, c1=c1: e.dma_start(out=at_raw[:, :, c0 * N:c1 * N], in_=at_v[:, :, c0 * N:c1 * N]))
+        for ps in range(4):
+            add("Lb%d" % ps, [], lambda e, ps=ps: e.dma_start(out=b_raw[:, ps, :, :], in_=b_src(ps)))
+            for s in range(2):
+                add("Lb%d%d" % (ps, s), [], lambda e, ps=ps, s=s: e.dma_start(out=b_raw[:, ps, :, cols(s)], in_=b_src(ps)[:, :, cols(s)]))
+        for g in range(3):
+            add("Lw%d" % g, [], lambda e, g=g: e.dma_start(out=w_raw[:, g, :].bitcast(I32), in_=wt_words[g].bitcast(I32)))
+            for hf in range(2):
+                add("Lw%d%s" % (g, "AB"[hf]), [], lambda e, g=g, hf=hf: e.dma_start(out=w_raw[:, g, cols(hf, R)].bitcast(I32), in_=wt_words[g][:, cols(hf, R)].bitcast(I32)))
+        add("LwB", [], lambda e: e.dma_start(out=w_raw[:, :, cols(1, R)].bitcast(I32), in_=wt_words.rearrange("g p n -> p g n")[:, :, cols(1, R)].bitcast(I32)))
+        add("zs", [], lambda e: e.memset(ws_raw[:].rearrange("p g r -> p (g r)").bitcast(I32), 0))
+        for q in range(4):
+            add("Lsc%d" % q, ["zs"], lambda e, q=q: e.dma_start(
+                out=ws_raw[32 * q:32 * q + 4, :, :].bitcast(I32),
+                in_=wt_scales[:, 4 * q:4 * q + 4, :].rearrange("g r n -> r g n").bitcast(I32)))
+        add("Lrho", [], lambda e: e.dma_start(out=rho_sb[:], in_=rho.rearrange("(g p t) -> p g t", g=4, t=4)))
+        for G in range(4):
+            h_v = h[cols(G), :].rearrange("(p t) s -> p t s", t=4)
+            add("Lh%d" % G, [], lambda e, G=G, h_v=h_v: e.dma_start(out=h_sb[:, G, :, :], in_=h_v))
+            for s in range(2):
+                add("Lh%d%d" % (G, s), [], lambda e, G=G, s=s, h_v=h_v: e.dma_start(out=h_sb[:, G, :, cols(s)], in_=h_v[:, :, cols(s)]))
+
+        queued = set(Q_SYNC + Q_ACT + Q_DVE + Q_POOL + Q_PE)
+
+        def pick(*names):
+            return [n for n in names if n in queued][:1]
+
+        def copy(e, out, in_):
+            if e is nc.scalar:
+                e.copy(out=out, in_=in_)
+            else:
+                e.tensor_copy(out=out, in_=in_)
+
+        def interleave(e, key, src, c0=0, c1=N):
+            if key not in grouped:
+                grouped[key] = stage.tile([P, N, 4], BF16, align_bytes=64, name="grouped")
+            copy(e, grouped[key][:, c0:c1, :].rearrange("p (c i) t -> p c t i", i=4), src[:, :, c0:c1].rearrange("p t (c i) -> p c t i", i=4))
+
+        def interleave_at(e, G):
+            grouped["a%d" % G] = stage.tile([P, N, 4], BF16, align_bytes=64, name="grouped")
+            dst = grouped["a%d" % G][:].rearrange("p (t c i) j -> p c t i j", t=4, i=2)
+            copy(e, dst, at_raw[:, :, cols(G)].rearrange("p j (c i t) -> p c t i j", t=4, i=2))
+
+        def quantize(key, codes, scales, c0=0, c1=N):
+            nc.vector.quantize_mx(out=codes[:, c0:c1].bitcast(FP8X4), scales=scales[:, c0:c1], in_=grouped[key][:, c0:c1, :].rearrange("p n j -> p (n j)"))
+
+        for G in range(4):
+            add("ia%d" % G, pick("Lat%d" % G, "Lat01" if G < 2 else "Lat23"), lambda e, G=G: interleave_at(e, G))
+            add("qa%d" % G, ["ia%d" % G], lambda e, G=G: quantize("a%d" % G, a_codes[:, G, :], a_scales[:, G, :]))
+            add("sp%d" % G, ["Lsc0", "Lsc1", "Lsc2", "Lsc3"], lambda e, G=G: e.tensor_copy(
+                out=w_scales[:, G, :, :].rearrange("p g (t m) -> p t g m", t=4),
+                in_=ws_raw[:, :, cols(G)].rearrange("p g (m t) -> p t g m", t=4)))
+            for g in range(3):
+                add("wp%d%d" % (g, G), pick("Lw%d" % g, "Lw%d%s" % (g, "AB"[G // 2]), "LwB"), lambda e, G=G, g=g: e.tensor_copy(
+                    out=w_codes[:, G, g, :].rearrange("p (t m b) -> p t m b", t=4, b=2),
+                    in_=w_raw[:, g, cols(G, 2 * N)].rearrange("p (m t b) -> p t m b", t=4, b=2)))
+        for ps in range(4):
+            for s in range(2):
+                ld = pick("Lb%d%d" % (ps, s), "Lb%d" % ps)
+                key = "b%d%d" % (ps, s)
+                add("i" + key, ld, lambda e, ps=ps, s=s, key=key: interleave(e, key, b_raw[:, ps, :, cols(s)]))
+                add("i" + key + "L", ld, lambda e, ps=ps, s=s, key=key: interleave(e, key, b_raw[:, ps, :, cols(s)], 0, 320))
+                add("i" + key + "R", ld, lambda e, ps=ps, s=s, key=key: interleave(e, key, b_raw[:, ps, :, cols(s)], 320, N))
+                add("q" + key, [n for n in ("i" + key, "i" + key + "L", "i" + key + "R") if n in queued],
+                    lambda e, ps=ps, s=s, key=key: quantize(key, b_codes[:, ps, cols(s)], b_scales[:, ps, cols(s)]))
+
+        def mm(k, t, ps):
+            G, s = UNITS[k]
+            if ps == 0:
+                acc[k, t] = psum.tile([P, N], F32, name="acc")
+                lhs = a_codes[:, G, cols(t, P)].bitcast(FP8X4)
+                lhs_scale = a_scales[:, G, cols(t, P)]
+            else:
+                lhs = w_codes[:, G, ps - 1, cols(t, 2 * P)].bitcast(FP4X4)
+                lhs_scale = w_scales[:, G, ps - 1, cols(t, P)]
+            nc.tensor.matmul_mx(out=acc[k, t][:], lhsT=lhs, lhsT_scale=lhs_scale, rhs=b_codes[:, ps, cols(s)].bitcast(FP8X4),
+                                rhs_scale=b_scales[:, ps, cols(s)], start=(ps == 0), stop=(ps == 3))
+
+        def sub(e, k, t, c0=0, c1=N):
+            G, s = UNITS[k]
+            if k not in ytile:
+                ytile[k] = ypool.tile([P, 4, N], F32, align_bytes=64, name="y")
+            e.tensor_tensor(out=ytile[k][:, t, c0:c1], in0=acc[k, t][:, c0:c1], in1=h_sb[:, G, t, s * N + c0:s * N + c1], op=ALU.subtract)
+
+        def relu(e, k, t, c0=0, c1=N):
+            G, s = UNITS[k]
+            e.tensor_scalar(out=ytile[k][:, t, c0:c1], in0=ytile[k][:, t, c0:c1], scalar1=0.0, scalar2=rho_sb[:, G, t:t + 1], op0=ALU.max, op1=ALU.mult)
+
+        def quantize_y(k, c0=0, c1=N):
+            G, s = UNITS[k]
+            if k not in ycodes:
+                ycodes[k] = cpool.tile([P, N], U32, align_bytes=64, name="ycodes")
+            quantize("o%d" % k, ycodes[k], y_scales[4 * G:, cols(s)], c0, c1)
+
+        for k in range(8):
+            G, s = UNITS[k]
+            y_v = out_0[cols(G), cols(s)].rearrange("(p t) m -> p t m", t=4)
+            for t in range(4):
+                for ps in range(4):
+                    deps = ["qa%d" % G, "qb0%d" % s] if ps == 0 else ["m%d%d%d" % (k, t, ps - 1), "qb%d%d" % (ps, s), "wp%d%d" % (ps - 1, G), "sp%d" % G]
+                    add("m%d%d%d" % (k, t, ps), deps, lambda e, k=k, t=t, ps=ps: mm(k, t, ps))
+                sdeps = ["m%d%d3" % (k, t)] + pick("Lh%d%d" % (G, s), "Lh%d" % G)
+                add("s%d%d" % (k, t), sdeps, lambda e, k=k, t=t: sub(e, k, t))
+                add("r%d%d" % (k, t), ["s%d%d" % (k, t), "Lrho"], lambda e, k=k, t=t: relu(e, k, t))
+                add("Sy%d%d" % (k, t), ["r%d%d" % (k, t)], lambda e, k=k, t=t, y_v=y_v: e.dma_start(out=y_v[:, t, :], in_=ytile[k][:, t, :]))
+            rs = ["r%d%d" % (k, t) for t in range(4)]
+            add("Sy%d" % k, rs, lambda e, k=k, y_v=y_v: e.dma_start(out=y_v, in_=ytile[k][:]))
+            add("io%d" % k, rs, lambda e, k=k: interleave(e, "o%d" % k, ytile[k]))
+            add("io%dL" % k, rs, lambda e, k=k: interleave(e, "o%d" % k, ytile[k], 0, 256))
+            add("io%dR" % k, rs, lambda e, k=k: interleave(e, "o%d" % k, ytile[k], 256, N))
+            add("qo%d" % k, ["io%d" % k], lambda e, k=k: quantize_y(k))
+            add("qo%dL" % k, ["io%dL" % k], lambda e, k=k: quantize_y(k, 0, 256))
+            add("qo%dR" % k, ["io%dR" % k], lambda e, k=k: quantize_y(k, 256, N))
+            qs = [n for n in ("qo%d" % k, "qo%dL" % k, "qo%dR" % k) if n in queued]
+            add("Sc%d" % k, qs, lambda e, k=k, G=G, s=s: e.dma_start(
+                out=out_1[G][:, cols(s), :].rearrange("p m t -> p (m t)").bitcast(I32), in_=ycodes[k][:].bitcast(I32)))
+        all_q = [n for n in queued if n.startswith("qo")]
+        for q in range(4):
+            add("Ss%d" % q, all_q, lambda e, q=q: e.dma_start(
+                out=out_2[:, 4 * q:4 * q + 4, :].bitcast(I32), in_=y_scales[32 * q:32 * q + 16, :].bitcast(I32)))
+
+        queues = [(nc.sync, Q_SYNC), (nc.scalar, Q_ACT), (nc.vector, Q_DVE), (nc.gpsimd, Q_POOL), (nc.tensor, Q_PE)]
+        pos = [0] * len(queues)
+        done = set()
+        ctx.enter_context(tc.manual_schedule())
+        while any(pos[i] < len(queues[i][1]) for i in range(len(queues))):
+            moved = False
+            for i in range(len(queues)):
+                e, names = queues[i]
+                if pos[i] < len(names) and all(d in done for d in steps[names[pos[i]]][0]):
+                    steps[names[pos[i]]][1](e)
+                    done.add(names[pos[i]])
+                    pos[i] += 1
+                    moved = True
+            assert moved

@@ -17,11 +17,11 @@ ALU = mybir.AluOpType
 P = 128
 N = 512
 UNITS = [[0,0],[1,0],[2,0],[3,0],[0,1],[1,1],[2,1],[3,1]]
-Q_SYNC = "Lat0 Lw0 Lb00 Lsc0 Lsc1 Lsc2 Lsc3 Lb10 Lw1 Lb20 Lb30 Lw2 Lat1 Lh0 Lat23 Lh1 Lb01 Lb11 Lh2 Lb21 Lb31 Lh3 Sy0 Sy1 Sy2 Sy3 Sc0 Sc1 Sy4 Sc2 Sc3 Sy5 Sc4 Sy6 Sc5 Sy70 Sy71 Sy72 Sc6 Sy73 Sc7 Ss0 Ss1".split()
-Q_ACT = "Lrho ib00 ib10 ib20 ib30 ia1 ia2 ia3 ib01 ib11 ib21 ib31 io0 io1 io2 io3 io4 io5 io6 io7R Ss2 Ss3".split()
-Q_DVE = "zs ia0 qa0 wp00 wp01 wp02 wp03 qb00 sp0 sp1 sp2 sp3 qb10 wp10 wp11 qb20 wp12 wp13 wp20 wp21 qb30 wp22 s00 s01 r00 qa1 s02 r01 wp23 s03 r02 r03 s10 s11 r10 qa2 s12 r11 s13 r12 qa3 r13 s20 s21 r20 qb01 s22 r21 s23 r22 qb11 r23 s30 s31 r30 qb21 s32 r31 s33 r32 qb31 r33 s40 s41 r40 qo0 s42 r41 qo1 s43 r42 r43 qo2 s50 s51 r50 qo3 s52 r51 s53 r52 qo4 r53 s60 s61 r60 s62 r61 s63 r62 qo5 r63 s70 s71 r70 s72 r71 qo6 s73 r72 r73 io7L qo7L qo7R".split()
-Q_POOL = "".split()
-Q_PE = "m000 m010 m020 m030 m001 m011 m021 m031 m002 m012 m022 m032 m003 m013 m023 m033 m100 m101 m102 m103 m110 m111 m112 m113 m120 m121 m122 m123 m130 m131 m132 m133 m200 m201 m202 m203 m210 m211 m212 m213 m220 m221 m222 m223 m230 m231 m232 m233 m300 m301 m302 m303 m310 m311 m312 m313 m320 m321 m322 m323 m330 m331 m332 m333 m400 m401 m402 m403 m410 m411 m412 m413 m420 m421 m422 m423 m430 m431 m432 m433 m500 m501 m502 m503 m510 m511 m512 m513 m520 m521 m522 m523 m530 m531 m532 m533 m600 m601 m602 m603 m610 m611 m612 m613 m620 m621 m622 m623 m630 m631 m632 m633 m700 m701 m702 m703 m710 m711 m712 m713 m720 m721 m722 m723 m730 m731 m732 m733".split()
+Q_SYNC = "Lat0 Lw0 Lb00 Lb10 Lat1 Lw1 Mv10 Mv11 Mv12 Mv13 Lb20 Lw2 Mv20 Mv21 Mv22 Mv23 Lb30 Lh0 Lat23 Lh1 Lb01 Lb11 Lh2 Lb21 Lb31 Lh3 Sy0 Sy1 Sy2 Sy3 Sc0 Sc1 Sy4 Sc2 Sc3 Sy5 Sc4 Sy6 Sc5 Sy70 Sy71 Sy72 Sc6 Sy73 Sc7 Ss0 Ss1".split()
+Q_ACT = "Lsc0 Lsc1 Lsc2 Lsc3 Lrho ib00 ib10 ib20 ib30R ia2 ia3 ib01 ib11 ib21 ib31 io0 io1 io2 io3 io4 io5 io6 io7R Ss2 Ss3".split()
+Q_DVE = "ia0 qa0 wp00 wp01 sp wp02 wp03 qb00 ia1 qb10 wp10 qa1 wp11 wp12 wp13 qb20 wp20 wp21 ib30L wp22 qb30 wp23 s00 s01 r00 s02 r01 s03 r02 r03 qa2 s10 s11 r10 s12 r11 qa3 s13 r12 r13 s20 s21 r20 qb01 s22 r21 s23 r22 qb11 r23 s30 s31 r30 qb21 s32 r31 s33 r32 qb31 r33 s40 s41 r40 qo0 s42 r41 qo1 s43 r42 r43 qo2 s50 s51 r50 qo3 s52 r51 s53 r52 qo4 r53 s60 s61 r60 s62 r61 s63 r62 qo5 r63 s70 s71 r70 s72 r71 qo6 s73 r72 r73 io7L qo7L qo7R".split()
+Q_POOL = "zs zp1 zp2".split()
+Q_PE = "m000 m010 m020 m030 m001 m011 m021 m031 m100 m110 m120 m130 m101 m111 m121 m131 m002 m012 m022 m032 m102 m112 m122 m132 m003 m013 m023 m033 m103 m113 m123 m133 m200 m201 m202 m203 m210 m211 m212 m213 m220 m221 m222 m223 m230 m231 m232 m233 m300 m301 m302 m303 m310 m311 m312 m313 m320 m321 m322 m323 m330 m331 m332 m333 m400 m410 m420 m430 m401 m411 m421 m431 m402 m412 m422 m432 m403 m413 m423 m433 m500 m501 m502 m503 m510 m511 m512 m513 m520 m521 m522 m523 m530 m531 m532 m533 m600 m601 m602 m603 m610 m611 m612 m613 m620 m621 m622 m623 m630 m631 m632 m633 m700 m701 m702 m703 m710 m711 m712 m713 m720 m721 m722 m723 m730 m731 m732 m733".split()
 
 
 def tile_two_stage_penalty_violation_g5_kernel(tc, at, x, wt_words, wt_scales, u, h, rho, out_0, out_1, out_2):
@@ -37,9 +37,9 @@ def tile_two_stage_penalty_violation_g5_kernel(tc, at, x, wt_words, wt_scales, u
         b_raw = keep.tile([P, 4, 4, S], BF16, align_bytes=64)
         h_sb = keep.tile([P, 4, 4, S], BF16, align_bytes=64)
         w_raw = keep.tile([P, 3, 2 * R], U8, align_bytes=64)
-        ws_raw = keep.tile([P, 3, R], U8, align_bytes=64)
+        ws_raw = keep.tile([P, R], U8, align_bytes=64)
         w_codes = keep.tile([P, 4, 3, 2 * N], U8, align_bytes=64)
-        w_scales = keep.tile([P, 4, 3, N], U8, align_bytes=64)
+        w_scales = [keep.tile([P, R], U8, align_bytes=64, name="w_scales%d" % g) for g in range(3)]
         a_codes = keep.tile([P, 4, N], U32, align_bytes=64)
         a_scales = keep.tile([P, 4, N], U8, align_bytes=64)
         b_codes = keep.tile([P, 4, S], U32, align_bytes=64)
@@ -75,11 +75,20 @@ def tile_two_stage_penalty_violation_g5_kernel(tc, at, x, wt_words, wt_scales, u
             for hf in range(2):
                 add("Lw%d%s" % (g, "AB"[hf]), [], lambda e, g=g, hf=hf: e.dma_start(out=w_raw[:, g, cols(hf, R)].bitcast(I32), in_=wt_words[g][:, cols(hf, R)].bitcast(I32)))
         add("LwB", [], lambda e: e.dma_start(out=w_raw[:, :, cols(1, R)].bitcast(I32), in_=wt_words.rearrange("g p n -> p g n")[:, :, cols(1, R)].bitcast(I32)))
-        add("zs", [], lambda e: e.memset(ws_raw[:].rearrange("p g r -> p (g r)").bitcast(I32), 0))
+        add("zs", [], lambda e: e.memset(ws_raw[:].bitcast(I32), 0))
+        add("zp1", [], lambda e: e.memset(w_scales[1][:].bitcast(I32), 0))
+        add("zp2", [], lambda e: e.memset(w_scales[2][:].bitcast(I32), 0))
+        add("sp", ["Lsc0", "Lsc1", "Lsc2", "Lsc3"], lambda e: e.tensor_copy(
+            out=w_scales[0][:].rearrange("p (G t m) -> p G t m", G=4, t=4),
+            in_=ws_raw[:].rearrange("p (G m t) -> p G t m", G=4, t=4)))
+        for g in (1, 2):
+            for q in range(4):
+                add("Mv%d%d" % (g, q), ["sp", "zp%d" % g], lambda e, g=g, q=q: e.dma_start(
+                    out=w_scales[g][32 * q:32 * q + 4, :].bitcast(I32), in_=w_scales[0][32 * q + 4 * g:32 * q + 4 * g + 4, :].bitcast(I32)))
         for q in range(4):
             add("Lsc%d" % q, ["zs"], lambda e, q=q: e.dma_start(
-                out=ws_raw[32 * q:32 * q + 4, :, :].bitcast(I32),
-                in_=wt_scales[:, 4 * q:4 * q + 4, :].rearrange("g r n -> r g n").bitcast(I32)))
+                out=ws_raw[32 * q:32 * q + 12, :].bitcast(I32),
+                in_=wt_scales[:, 4 * q:4 * q + 4, :].bitcast(I32)))
         add("Lrho", [], lambda e: e.dma_start(out=rho_sb[:], in_=rho.rearrange("(g p t) -> p g t", g=4, t=4)))
         for G in range(4):
             h_v = h[cols(G), :].rearrange("(p t) s -> p t s", t=4)
@@ -114,9 +123,6 @@ def tile_two_stage_penalty_violation_g5_kernel(tc, at, x, wt_words, wt_scales, u
         for G in range(4):
             add("ia%d" % G, pick("Lat%d" % G, "Lat01" if G < 2 else "Lat23"), lambda e, G=G: interleave_at(e, G))
             add("qa%d" % G, ["ia%d" % G], lambda e, G=G: quantize("a%d" % G, a_codes[:, G, :], a_scales[:, G, :]))
-            add("sp%d" % G, ["Lsc0", "Lsc1", "Lsc2", "Lsc3"], lambda e, G=G: e.tensor_copy(
-                out=w_scales[:, G, :, :].rearrange("p g (t m) -> p t g m", t=4),
-                in_=ws_raw[:, :, cols(G)].rearrange("p g (m t) -> p t g m", t=4)))
             for g in range(3):
                 add("wp%d%d" % (g, G), pick("Lw%d" % g, "Lw%d%s" % (g, "AB"[G // 2]), "LwB"), lambda e, G=G, g=g: e.tensor_copy(
                     out=w_codes[:, G, g, :].rearrange("p (t m b) -> p t m b", t=4, b=2),
@@ -139,7 +145,7 @@ def tile_two_stage_penalty_violation_g5_kernel(tc, at, x, wt_words, wt_scales, u
                 lhs_scale = a_scales[:, G, cols(t, P)]
             else:
                 lhs = w_codes[:, G, ps - 1, cols(t, 2 * P)].bitcast(FP4X4)
-                lhs_scale = w_scales[:, G, ps - 1, cols(t, P)]
+                lhs_scale = w_scales[ps - 1][:, cols(4 * G + t, P)]
             nc.tensor.matmul_mx(out=acc[k, t][:], lhsT=lhs, lhsT_scale=lhs_scale, rhs=b_codes[:, ps, cols(s)].bitcast(FP8X4),
                                 rhs_scale=b_scales[:, ps, cols(s)], start=(ps == 0), stop=(ps == 3))
 
@@ -164,7 +170,7 @@ def tile_two_stage_penalty_violation_g5_kernel(tc, at, x, wt_words, wt_scales, u
             y_v = out_0[cols(G), cols(s)].rearrange("(p t) m -> p t m", t=4)
             for t in range(4):
                 for ps in range(4):
-                    deps = ["qa%d" % G, "qb0%d" % s] if ps == 0 else ["m%d%d%d" % (k, t, ps - 1), "qb%d%d" % (ps, s), "wp%d%d" % (ps - 1, G), "sp%d" % G]
+                    deps = ["qa%d" % G, "qb0%d" % s] if ps == 0 else ["m%d%d%d" % (k, t, ps - 1), "qb%d%d" % (ps, s), "wp%d%d" % (ps - 1, G), ["sp", "Mv13", "Mv23"][ps - 1]]
                     add("m%d%d%d" % (k, t, ps), deps, lambda e, k=k, t=t, ps=ps: mm(k, t, ps))
                 sdeps = ["m%d%d3" % (k, t)] + pick("Lh%d%d" % (G, s), "Lh%d" % G)
                 add("s%d%d" % (k, t), sdeps, lambda e, k=k, t=t: sub(e, k, t))

@@ -17,11 +17,11 @@ ALU = mybir.AluOpType
 P = 128
 N = 512
 UNITS = [[0,0],[1,0],[2,0],[3,0],[0,1],[1,1],[2,1],[3,1]]
-Q_SYNC = "Lat0 Lw0 Lb00 Lb10 Lat1 Lw1 Mv10 Mv11 Mv12 Mv13 Lb20 Lw2 Mv20 Mv21 Mv22 Mv23 Lb30 Lh0 Lat23 Lh1 Lb01 Lb11 Lh2 Lb21 Lb31 Lh3 Sy0 Sy1 Sy2 Sy3 Sc0 Sc1 Sy4 Sc2 Sc3 Sy5 Sc4 Sy6 Sc5 Sy70 Sy71 Sy72 Sc6 Sy73 Sc7 Ss0 Ss1".split()
-Q_ACT = "Lsc0 Lsc1 Lsc2 Lsc3 Lrho ib00 ib10 ib20 ib30R ia2 ia3 ib01 ib11 ib21 ib31 io0 io1 io2 io3 io4 io5 io6 io7R Ss2 Ss3".split()
-Q_DVE = "ia0 qa0 wp00 wp01 sp wp02 wp03 qb00 ia1 qb10 wp10 qa1 wp11 wp12 wp13 qb20 wp20 wp21 ib30L wp22 qb30 wp23 s00 s01 r00 s02 r01 s03 r02 r03 qa2 s10 s11 r10 s12 r11 qa3 s13 r12 r13 s20 s21 r20 qb01 s22 r21 s23 r22 qb11 r23 s30 s31 r30 qb21 s32 r31 s33 r32 qb31 r33 s40 s41 r40 qo0 s42 r41 qo1 s43 r42 r43 qo2 s50 s51 r50 qo3 s52 r51 s53 r52 qo4 r53 s60 s61 r60 s62 r61 s63 r62 qo5 r63 s70 s71 r70 s72 r71 qo6 s73 r72 r73 io7L qo7L qo7R".split()
+Q_SYNC = "Lw0A Lw0B Lat0 Lb00 Lw1 Lb10 Lat1 Mv10 Lw2 Mv11 Mv12 Lb20 Mv13 Mv20 Lb30 Mv21 Mv22 Lh00 Mv23 Lat23 Lh1 Lb01 Lb11 Lh2 Lb21 Lb31 Lh3 Lh01 Sy0 Sy1 Sy2 Sy3 Sc0 Sc1 Sy4 Sc2 Sc3 Ss00 Ss10 Sy5 Ss20 Ss30 Sc4 Sy6 Sc5 Sy70 Sy71 Sy72 Sc6 Sy73 Sc7 Ss01 Ss11".split()
+Q_ACT = "Lsc0 Lsc1 Lsc2 Lsc3 Lrho ib00 ib10 ia1 ib20 ib30R ia2 ia3 ib01 ib11 ib21 ib31 io0 io1 io2 io3 io4 io5 io6 io7R Ss21 Ss31".split()
+Q_DVE = "wp0A wp0B ia0 sp qa0 qb00 wp1A wp1B qb10 wp2A qa1 ib30L qb20 qb30 wp2B s00 s01 r00 s02 r01 s03 r02 r03 qa2 s10 s11 r10 s12 r11 qa3 s13 r12 r13 s20 s21 r20 qb01 s22 r21 s23 r22 qb11 r23 s30 s31 r30 qb21 s32 r31 s33 r32 qb31 r33 s40 s41 r40 qo0 s42 r41 qo1 s43 r42 r43 qo2 s50 s51 r50 qo3 s52 r51 s53 r52 qo4 r53 s60 s61 r60 s62 r61 s63 r62 qo5 r63 s70 s71 r70 s72 r71 qo6 s73 r72 r73 io7L qo7L qo7R".split()
 Q_POOL = "zs zp1 zp2".split()
-Q_PE = "m000 m010 m020 m030 m001 m011 m021 m031 m100 m110 m120 m130 m101 m111 m121 m131 m002 m012 m022 m032 m102 m112 m122 m132 m003 m013 m023 m033 m103 m113 m123 m133 m200 m201 m202 m203 m210 m211 m212 m213 m220 m221 m222 m223 m230 m231 m232 m233 m300 m301 m302 m303 m310 m311 m312 m313 m320 m321 m322 m323 m330 m331 m332 m333 m400 m410 m420 m430 m401 m411 m421 m431 m402 m412 m422 m432 m403 m413 m423 m433 m500 m501 m502 m503 m510 m511 m512 m513 m520 m521 m522 m523 m530 m531 m532 m533 m600 m601 m602 m603 m610 m611 m612 m613 m620 m621 m622 m623 m630 m631 m632 m633 m700 m701 m702 m703 m710 m711 m712 m713 m720 m721 m722 m723 m730 m731 m732 m733".split()
+Q_PE = "m000 m010 m020 m030 m001 m011 m021 m031 m100 m110 m120 m130 m101 m111 m121 m131 m002 m012 m022 m032 m003 m013 m023 m033 m102 m112 m122 m132 m103 m113 m123 m133 m200 m201 m202 m203 m210 m211 m212 m213 m220 m221 m222 m223 m230 m231 m232 m233 m300 m301 m302 m303 m310 m311 m312 m313 m320 m321 m322 m323 m330 m331 m332 m333 m400 m410 m420 m430 m401 m411 m421 m431 m402 m412 m422 m432 m403 m413 m423 m433 m500 m501 m502 m503 m510 m511 m512 m513 m520 m521 m522 m523 m530 m531 m532 m533 m600 m601 m602 m603 m610 m611 m612 m613 m620 m621 m622 m623 m630 m631 m632 m633 m700 m701 m702 m703 m710 m711 m712 m713 m720 m721 m722 m723 m730 m731 m732 m733".split()
 
 
 def tile_two_stage_penalty_violation_g5_kernel(tc, at, x, wt_words, wt_scales, u, h, rho, out_0, out_1, out_2):
@@ -84,7 +84,7 @@ def tile_two_stage_penalty_violation_g5_kernel(tc, at, x, wt_words, wt_scales, u
         for g in (1, 2):
             for q in range(4):
                 add("Mv%d%d" % (g, q), ["sp", "zp%d" % g], lambda e, g=g, q=q: e.dma_start(
-                    out=w_scales[g][32 * q:32 * q + 4, :].bitcast(I32), in_=w_scales[0][32 * q + 4 * g:32 * q + 4 * g + 4, :].bitcast(I32)))
+                    out=w_scales[g][q:128:32, :].bitcast(I32), in_=w_scales[0][4 * g + q:128:32, :].bitcast(I32)))
         for q in range(4):
             add("Lsc%d" % q, ["zs"], lambda e, q=q: e.dma_start(
                 out=ws_raw[32 * q:32 * q + 12, :].bitcast(I32),
@@ -107,10 +107,10 @@ def tile_two_stage_penalty_violation_g5_kernel(tc, at, x, wt_words, wt_scales, u
             else:
                 e.tensor_copy(out=out, in_=in_)
 
-        def interleave(e, key, src, c0=0, c1=N):
+        def interleave(e, key, src, c0=0, c1=N, run=4):
             if key not in grouped:
                 grouped[key] = stage.tile([P, N, 4], BF16, align_bytes=64, name="grouped")
-            copy(e, grouped[key][:, c0:c1, :].rearrange("p (c i) t -> p c t i", i=4), src[:, :, c0:c1].rearrange("p t (c i) -> p c t i", i=4))
+            copy(e, grouped[key][:, c0:c1, :].rearrange("p (c i) t -> p c t i", i=run), src[:, :, c0:c1].rearrange("p t (c i) -> p c t i", i=run))
 
         def interleave_at(e, G):
             grouped["a%d" % G] = stage.tile([P, N, 4], BF16, align_bytes=64, name="grouped")
@@ -127,6 +127,11 @@ def tile_two_stage_penalty_violation_g5_kernel(tc, at, x, wt_words, wt_scales, u
                 add("wp%d%d" % (g, G), pick("Lw%d" % g, "Lw%d%s" % (g, "AB"[G // 2]), "LwB"), lambda e, G=G, g=g: e.tensor_copy(
                     out=w_codes[:, G, g, :].rearrange("p (t m b) -> p t m b", t=4, b=2),
                     in_=w_raw[:, g, cols(G, 2 * N)].rearrange("p (m t b) -> p t m b", t=4, b=2)))
+        for g in range(3):
+            for hf in range(2):
+                add("wp%d%s" % (g, "AB"[hf]), pick("Lw%d" % g, "Lw%d%s" % (g, "AB"[hf])), lambda e, hf=hf, g=g: e.tensor_copy(
+                    out=w_codes[:, 2 * hf:2 * hf + 2, g, :].rearrange("p G (t m b) -> p G t m b", t=4, b=2),
+                    in_=w_raw[:, g, cols(hf, R)].rearrange("p (G m t b) -> p G t m b", G=2, t=4, b=2)))
         for ps in range(4):
             for s in range(2):
                 ld = pick("Lb%d%d" % (ps, s), "Lb%d" % ps)
@@ -152,7 +157,8 @@ def tile_two_stage_penalty_violation_g5_kernel(tc, at, x, wt_words, wt_scales, u
         def sub(e, k, t, c0=0, c1=N):
             G, s = UNITS[k]
             if k not in ytile:
-                ytile[k] = ypool.tile([P, 4, N], F32, align_bytes=64, name="y")
+                y_unit = ypool.tile([P, 4, N], F32, align_bytes=64, name="y")
+                ytile[k] = y_unit[:]
             e.tensor_tensor(out=ytile[k][:, t, c0:c1], in0=acc[k, t][:, c0:c1], in1=h_sb[:, G, t, s * N + c0:s * N + c1], op=ALU.subtract)
 
         def relu(e, k, t, c0=0, c1=N):
@@ -161,8 +167,9 @@ def tile_two_stage_penalty_violation_g5_kernel(tc, at, x, wt_words, wt_scales, u
 
         def quantize_y(k, c0=0, c1=N):
             G, s = UNITS[k]
-            if k not in ycodes:
-                ycodes[k] = cpool.tile([P, N], U32, align_bytes=64, name="ycodes")
+            if ("G", G) not in ycodes:
+                ycodes["G", G] = cpool.tile([P, S], U32, align_bytes=64, name="ycodes")
+            ycodes[k] = ycodes["G", G][:, cols(s)]
             quantize("o%d" % k, ycodes[k], y_scales[4 * G:, cols(s)], c0, c1)
 
         for k in range(8):
@@ -170,27 +177,37 @@ def tile_two_stage_penalty_violation_g5_kernel(tc, at, x, wt_words, wt_scales, u
             y_v = out_0[cols(G), cols(s)].rearrange("(p t) m -> p t m", t=4)
             for t in range(4):
                 for ps in range(4):
-                    deps = ["qa%d" % G, "qb0%d" % s] if ps == 0 else ["m%d%d%d" % (k, t, ps - 1), "qb%d%d" % (ps, s), "wp%d%d" % (ps - 1, G), ["sp", "Mv13", "Mv23"][ps - 1]]
+                    deps = ["qa%d" % G, "qb0%d" % s] if ps == 0 else ["m%d%d%d" % (k, t, ps - 1), "qb%d%d" % (ps, s), "wp%d%s" % (ps - 1, "AB"[G // 2]), ["sp", "Mv13", "Mv23"][ps - 1]]
                     add("m%d%d%d" % (k, t, ps), deps, lambda e, k=k, t=t, ps=ps: mm(k, t, ps))
                 sdeps = ["m%d%d3" % (k, t)] + pick("Lh%d%d" % (G, s), "Lh%d" % G)
                 add("s%d%d" % (k, t), sdeps, lambda e, k=k, t=t: sub(e, k, t))
                 add("r%d%d" % (k, t), ["s%d%d" % (k, t), "Lrho"], lambda e, k=k, t=t: relu(e, k, t))
                 add("Sy%d%d" % (k, t), ["r%d%d" % (k, t)], lambda e, k=k, t=t, y_v=y_v: e.dma_start(out=y_v[:, t, :], in_=ytile[k][:, t, :]))
             rs = ["r%d%d" % (k, t) for t in range(4)]
-            add("Sy%d" % k, rs, lambda e, k=k, y_v=y_v: e.dma_start(out=y_v, in_=ytile[k][:]))
-            add("io%d" % k, rs, lambda e, k=k: interleave(e, "o%d" % k, ytile[k]))
-            add("io%dL" % k, rs, lambda e, k=k: interleave(e, "o%d" % k, ytile[k], 0, 256))
-            add("io%dR" % k, rs, lambda e, k=k: interleave(e, "o%d" % k, ytile[k], 256, N))
+            add("Sy%d" % k, rs, lambda e, k=k, y_v=y_v: e.dma_start(out=y_v, in_=ytile[k]))
+            add("io%d" % k, rs, lambda e, k=k: interleave(e, "o%d" % k, ytile[k], 0, N, 2))
+            add("io%dL" % k, rs, lambda e, k=k: interleave(e, "o%d" % k, ytile[k], 0, 256, 2))
+            add("io%dR" % k, rs, lambda e, k=k: interleave(e, "o%d" % k, ytile[k], 256, N, 2))
             add("qo%d" % k, ["io%d" % k], lambda e, k=k: quantize_y(k))
             add("qo%dL" % k, ["io%dL" % k], lambda e, k=k: quantize_y(k, 0, 256))
             add("qo%dR" % k, ["io%dR" % k], lambda e, k=k: quantize_y(k, 256, N))
             qs = [n for n in ("qo%d" % k, "qo%dL" % k, "qo%dR" % k) if n in queued]
             add("Sc%d" % k, qs, lambda e, k=k, G=G, s=s: e.dma_start(
-                out=out_1[G][:, cols(s), :].rearrange("p m t -> p (m t)").bitcast(I32), in_=ycodes[k][:].bitcast(I32)))
+                out=out_1[G][:, cols(s), :].rearrange("p m t -> p (m t)").bitcast(I32), in_=ycodes[k].bitcast(I32)))
+        for G in range(4):
+            ks = [k for k in range(8) if UNITS[k][0] == G]
+            add("SY%d" % G, ["r%d%d" % (k, t) for k in ks for t in range(4)], lambda e, G=G: e.dma_start(
+                out=out_0[cols(G), :].rearrange("(p t) m -> p t m", t=4), in_=ytile["G", G][:]))
+            add("SC%d" % G, ["qo%d" % k for k in ks], lambda e, G=G: e.dma_start(
+                out=out_1[G].rearrange("p m t -> p (m t)").bitcast(I32), in_=ycodes["G", G][:].bitcast(I32)))
         all_q = [n for n in queued if n.startswith("qo")]
         for q in range(4):
             add("Ss%d" % q, all_q, lambda e, q=q: e.dma_start(
                 out=out_2[:, 4 * q:4 * q + 4, :].bitcast(I32), in_=y_scales[32 * q:32 * q + 16, :].bitcast(I32)))
+
+            for s in range(2):
+                add("Ss%d%d" % (q, s), [n for n in all_q if UNITS[int(n[2])][1] == s], lambda e, q=q, s=s: e.dma_start(
+                    out=out_2[:, 4 * q:4 * q + 4, cols(s)].bitcast(I32), in_=y_scales[32 * q:32 * q + 16, cols(s)].bitcast(I32)))
 
         queues = [(nc.sync, Q_SYNC), (nc.scalar, Q_ACT), (nc.vector, Q_DVE), (nc.gpsimd, Q_POOL), (nc.tensor, Q_PE)]
         pos = [0] * len(queues)

from contextlib import ExitStack

import concourse.mybir as mybir

R, S, K1, K2 = 2048, 1024, 512, 1536
FLOPS = 2 * R * S * (K1 + K2)

F32 = mybir.dt.float32
BF16 = mybir.dt.bfloat16
I32 = mybir.dt.int32
U32 = mybir.dt.uint32
U8 = mybir.dt.uint8
FP8X4 = mybir.dt.float8_e4m3fn_x4
FP4X4 = mybir.dt.float4_e2m1fn_x4
ALU = mybir.AluOpType

P = 128
N = 512
UNITS = [[0,0],[1,0],[2,0],[3,0],[0,1],[1,1],[2,1],[3,1]]
Q_SYNC = "Lw0A Lw0B Lat0 Lb00 Lw1 Lb10 Lat1 Mv10 Lw2 Mv11 Mv12 Lb20 Mv13 Mv20 Lb30 Mv21 Mv22 Lh00 Mv23 Lat23 Lh1 Lb01 Lb11 Lh2 Lb21 Lb31 Lh3 Lh01 Sy0 Sy1 Sy2 Sy3 Sc0 Sc1 Sy4 Sc2 Sc3 Ss00 Ss10 Sy5 Ss20 Ss30 Sc4 Sy6 Sc5 Sy70 Sy71 Sy72 Sc6 Sy73 Sc7 Ss01 Ss11".split()
Q_ACT = "Lsc0 Lsc1 Lsc2 Lsc3 Lrho ib00 ib10 ia1 ib20 ib30R ia2 ia3 ib01 ib11 ib21 ib31 io0 io1 io2 io3 io4 io5 io6 io7R Ss21 Ss31".split()
Q_DVE = "wp0A wp0B ia0 sp qa0 qb00 wp1A wp1B qb10 wp2A qa1 ib30L qb20 qb30 wp2B s00 s01 r00 s02 r01 s03 r02 r03 qa2 s10 s11 r10 s12 r11 qa3 s13 r12 r13 s20 s21 r20 qb01 s22 r21 s23 r22 qb11 r23 s30 s31 r30 qb21 s32 r31 s33 r32 qb31 r33 s40 s41 r40 qo0 s42 r41 qo1 s43 r42 r43 qo2 s50 s51 r50 qo3 s52 r51 s53 r52 qo4 r53 s60 s61 r60 s62 r61 s63 r62 qo5 r63 s70 s71 r70 s72 r71 qo6 s73 r72 r73 io7L qo7L qo7R".split()
Q_POOL = "zs zp1 zp2".split()
Q_PE = "m000 m010 m020 m030 m001 m011 m021 m031 m100 m110 m120 m130 m101 m111 m121 m131 m002 m012 m022 m032 m003 m013 m023 m033 m102 m112 m122 m132 m103 m113 m123 m133 m200 m201 m202 m203 m210 m211 m212 m213 m220 m221 m222 m223 m230 m231 m232 m233 m300 m301 m302 m303 m310 m311 m312 m313 m320 m321 m322 m323 m330 m331 m332 m333 m400 m410 m420 m430 m401 m411 m421 m431 m402 m412 m422 m432 m403 m413 m423 m433 m500 m501 m502 m503 m510 m511 m512 m513 m520 m521 m522 m523 m530 m531 m532 m533 m600 m601 m602 m603 m610 m611 m612 m613 m620 m621 m622 m623 m630 m631 m632 m633 m700 m701 m702 m703 m710 m711 m712 m713 m720 m721 m722 m723 m730 m731 m732 m733".split()


def tile_two_stage_penalty_violation_g5_kernel(tc, at, x, wt_words, wt_scales, u, h, rho, out_0, out_1, out_2):
    nc = tc.nc
    with ExitStack() as ctx:
        keep = ctx.enter_context(tc.tile_pool(name="keep", bufs=1))
        stage = ctx.enter_context(tc.tile_pool(name="stage", bufs=4))
        ypool = ctx.enter_context(tc.tile_pool(name="ypool", bufs=6))
        cpool = ctx.enter_context(tc.tile_pool(name="cpool", bufs=4))
        psum = ctx.enter_context(tc.psum_pool(name="psum", bufs=8))

        at_raw = keep.tile([P, 4, R], BF16, align_bytes=64)
        b_raw = keep.tile([P, 4, 4, S], BF16, align_bytes=64)
        h_sb = keep.tile([P, 4, 4, S], BF16, align_bytes=64)
        w_raw = keep.tile([P, 3, 2 * R], U8, align_bytes=64)
        ws_raw = keep.tile([P, R], U8, align_bytes=64)
        w_codes = keep.tile([P, 4, 3, 2 * N], U8, align_bytes=64)
        w_scales = [keep.tile([P, R], U8, align_bytes=64, name="w_scales%d" % g) for g in range(3)]
        a_codes = keep.tile([P, 4, N], U32, align_bytes=64)
        a_scales = keep.tile([P, 4, N], U8, align_bytes=64)
        b_codes = keep.tile([P, 4, S], U32, align_bytes=64)
        b_scales = keep.tile([P, 4, S], U8, align_bytes=64)
        y_scales = keep.tile([P, S], U8, align_bytes=64)
        rho_sb = keep.tile([P, 4, 4], BF16, align_bytes=64)

        grouped = {}
        acc = {}
        ytile = {}
        ycodes = {}
        steps = {}

        def cols(i, w=N):
            return slice(i * w, (i + 1) * w)

        def b_src(ps):
            src = x if ps == 0 else u[cols(ps - 1), :]
            return src.rearrange("(p j) s -> p j s", j=4)

        def add(name, deps, fn):
            steps[name] = (deps, fn)

        at_v = at.rearrange("(p j) r -> p j r", j=4)
        for name, c0, c1 in [("0", 0, 1), ("1", 1, 2), ("2", 2, 3), ("3", 3, 4), ("01", 0, 2), ("23", 2, 4)]:
            add("Lat" + name, [], lambda e, c0=c0, c1=c1: e.dma_start(out=at_raw[:, :, c0 * N:c1 * N], in_=at_v[:, :, c0 * N:c1 * N]))
        for ps in range(4):
            add("Lb%d" % ps, [], lambda e, ps=ps: e.dma_start(out=b_raw[:, ps, :, :], in_=b_src(ps)))
            for s in range(2):
                add("Lb%d%d" % (ps, s), [], lambda e, ps=ps, s=s: e.dma_start(out=b_raw[:, ps, :, cols(s)], in_=b_src(ps)[:, :, cols(s)]))
        for g in range(3):
            add("Lw%d" % g, [], lambda e, g=g: e.dma_start(out=w_raw[:, g, :].bitcast(I32), in_=wt_words[g].bitcast(I32)))
            for hf in range(2):
                add("Lw%d%s" % (g, "AB"[hf]), [], lambda e, g=g, hf=hf: e.dma_start(out=w_raw[:, g, cols(hf, R)].bitcast(I32), in_=wt_words[g][:, cols(hf, R)].bitcast(I32)))
        add("LwB", [], lambda e: e.dma_start(out=w_raw[:, :, cols(1, R)].bitcast(I32), in_=wt_words.rearrange("g p n -> p g n")[:, :, cols(1, R)].bitcast(I32)))
        add("zs", [], lambda e: e.memset(ws_raw[:].bitcast(I32), 0))
        add("zp1", [], lambda e: e.memset(w_scales[1][:].bitcast(I32), 0))
        add("zp2", [], lambda e: e.memset(w_scales[2][:].bitcast(I32), 0))
        add("sp", ["Lsc0", "Lsc1", "Lsc2", "Lsc3"], lambda e: e.tensor_copy(
            out=w_scales[0][:].rearrange("p (G t m) -> p G t m", G=4, t=4),
            in_=ws_raw[:].rearrange("p (G m t) -> p G t m", G=4, t=4)))
        for g in (1, 2):
            for q in range(4):
                add("Mv%d%d" % (g, q), ["sp", "zp%d" % g], lambda e, g=g, q=q: e.dma_start(
                    out=w_scales[g][q:128:32, :].bitcast(I32), in_=w_scales[0][4 * g + q:128:32, :].bitcast(I32)))
        for q in range(4):
            add("Lsc%d" % q, ["zs"], lambda e, q=q: e.dma_start(
                out=ws_raw[32 * q:32 * q + 12, :].bitcast(I32),
                in_=wt_scales[:, 4 * q:4 * q + 4, :].bitcast(I32)))
        add("Lrho", [], lambda e: e.dma_start(out=rho_sb[:], in_=rho.rearrange("(g p t) -> p g t", g=4, t=4)))
        for G in range(4):
            h_v = h[cols(G), :].rearrange("(p t) s -> p t s", t=4)
            add("Lh%d" % G, [], lambda e, G=G, h_v=h_v: e.dma_start(out=h_sb[:, G, :, :], in_=h_v))
            for s in range(2):
                add("Lh%d%d" % (G, s), [], lambda e, G=G, s=s, h_v=h_v: e.dma_start(out=h_sb[:, G, :, cols(s)], in_=h_v[:, :, cols(s)]))

        queued = set(Q_SYNC + Q_ACT + Q_DVE + Q_POOL + Q_PE)

        def pick(*names):
            return [n for n in names if n in queued][:1]

        def copy(e, out, in_):
            if e is nc.scalar:
                e.copy(out=out, in_=in_)
            else:
                e.tensor_copy(out=out, in_=in_)

        def interleave(e, key, src, c0=0, c1=N, run=4):
            if key not in grouped:
                grouped[key] = stage.tile([P, N, 4], BF16, align_bytes=64, name="grouped")
            copy(e, grouped[key][:, c0:c1, :].rearrange("p (c i) t -> p c t i", i=run), src[:, :, c0:c1].rearrange("p t (c i) -> p c t i", i=run))

        def interleave_at(e, G):
            grouped["a%d" % G] = stage.tile([P, N, 4], BF16, align_bytes=64, name="grouped")
            dst = grouped["a%d" % G][:].rearrange("p (t c i) j -> p c t i j", t=4, i=2)
            copy(e, dst, at_raw[:, :, cols(G)].rearrange("p j (c i t) -> p c t i j", t=4, i=2))

        def quantize(key, codes, scales, c0=0, c1=N):
            nc.vector.quantize_mx(out=codes[:, c0:c1].bitcast(FP8X4), scales=scales[:, c0:c1], in_=grouped[key][:, c0:c1, :].rearrange("p n j -> p (n j)"))

        for G in range(4):
            add("ia%d" % G, pick("Lat%d" % G, "Lat01" if G < 2 else "Lat23"), lambda e, G=G: interleave_at(e, G))
            add("qa%d" % G, ["ia%d" % G], lambda e, G=G: quantize("a%d" % G, a_codes[:, G, :], a_scales[:, G, :]))
            for g in range(3):
                add("wp%d%d" % (g, G), pick("Lw%d" % g, "Lw%d%s" % (g, "AB"[G // 2]), "LwB"), lambda e, G=G, g=g: e.tensor_copy(
                    out=w_codes[:, G, g, :].rearrange("p (t m b) -> p t m b", t=4, b=2),
                    in_=w_raw[:, g, cols(G, 2 * N)].rearrange("p (m t b) -> p t m b", t=4, b=2)))
        for g in range(3):
            for hf in range(2):
                add("wp%d%s" % (g, "AB"[hf]), pick("Lw%d" % g, "Lw%d%s" % (g, "AB"[hf])), lambda e, hf=hf, g=g: e.tensor_copy(
                    out=w_codes[:, 2 * hf:2 * hf + 2, g, :].rearrange("p G (t m b) -> p G t m b", t=4, b=2),
                    in_=w_raw[:, g, cols(hf, R)].rearrange("p (G m t b) -> p G t m b", G=2, t=4, b=2)))
        for ps in range(4):
            for s in range(2):
                ld = pick("Lb%d%d" % (ps, s), "Lb%d" % ps)
                key = "b%d%d" % (ps, s)
                add("i" + key, ld, lambda e, ps=ps, s=s, key=key: interleave(e, key, b_raw[:, ps, :, cols(s)]))
                add("i" + key + "L", ld, lambda e, ps=ps, s=s, key=key: interleave(e, key, b_raw[:, ps, :, cols(s)], 0, 320))
                add("i" + key + "R", ld, lambda e, ps=ps, s=s, key=key: interleave(e, key, b_raw[:, ps, :, cols(s)], 320, N))
                add("q" + key, [n for n in ("i" + key, "i" + key + "L", "i" + key + "R") if n in queued],
                    lambda e, ps=ps, s=s, key=key: quantize(key, b_codes[:, ps, cols(s)], b_scales[:, ps, cols(s)]))

        def mm(k, t, ps):
            G, s = UNITS[k]
            if ps == 0:
                acc[k, t] = psum.tile([P, N], F32, name="acc")
                lhs = a_codes[:, G, cols(t, P)].bitcast(FP8X4)
                lhs_scale = a_scales[:, G, cols(t, P)]
            else:
                lhs = w_codes[:, G, ps - 1, cols(t, 2 * P)].bitcast(FP4X4)
                lhs_scale = w_scales[ps - 1][:, cols(4 * G + t, P)]
            nc.tensor.matmul_mx(out=acc[k, t][:], lhsT=lhs, lhsT_scale=lhs_scale, rhs=b_codes[:, ps, cols(s)].bitcast(FP8X4),
                                rhs_scale=b_scales[:, ps, cols(s)], start=(ps == 0), stop=(ps == 3))

        def sub(e, k, t, c0=0, c1=N):
            G, s = UNITS[k]
            if k not in ytile:
                y_unit = ypool.tile([P, 4, N], F32, align_bytes=64, name="y")
                ytile[k] = y_unit[:]
            e.tensor_tensor(out=ytile[k][:, t, c0:c1], in0=acc[k, t][:, c0:c1], in1=h_sb[:, G, t, s * N + c0:s * N + c1], op=ALU.subtract)

        def relu(e, k, t, c0=0, c1=N):
            G, s = UNITS[k]
            e.tensor_scalar(out=ytile[k][:, t, c0:c1], in0=ytile[k][:, t, c0:c1], scalar1=0.0, scalar2=rho_sb[:, G, t:t + 1], op0=ALU.max, op1=ALU.mult)

        def quantize_y(k, c0=0, c1=N):
            G, s = UNITS[k]
            if ("G", G) not in ycodes:
                ycodes["G", G] = cpool.tile([P, S], U32, align_bytes=64, name="ycodes")
            ycodes[k] = ycodes["G", G][:, cols(s)]
            quantize("o%d" % k, ycodes[k], y_scales[4 * G:, cols(s)], c0, c1)

        for k in range(8):
            G, s = UNITS[k]
            y_v = out_0[cols(G), cols(s)].rearrange("(p t) m -> p t m", t=4)
            for t in range(4):
                for ps in range(4):
                    deps = ["qa%d" % G, "qb0%d" % s] if ps == 0 else ["m%d%d%d" % (k, t, ps - 1), "qb%d%d" % (ps, s), "wp%d%s" % (ps - 1, "AB"[G // 2]), ["sp", "Mv13", "Mv23"][ps - 1]]
                    add("m%d%d%d" % (k, t, ps), deps, lambda e, k=k, t=t, ps=ps: mm(k, t, ps))
                sdeps = ["m%d%d3" % (k, t)] + pick("Lh%d%d" % (G, s), "Lh%d" % G)
                add("s%d%d" % (k, t), sdeps, lambda e, k=k, t=t: sub(e, k, t))
                add("r%d%d" % (k, t), ["s%d%d" % (k, t), "Lrho"], lambda e, k=k, t=t: relu(e, k, t))
                add("Sy%d%d" % (k, t), ["r%d%d" % (k, t)], lambda e, k=k, t=t, y_v=y_v: e.dma_start(out=y_v[:, t, :], in_=ytile[k][:, t, :]))
            rs = ["r%d%d" % (k, t) for t in range(4)]
            add("Sy%d" % k, rs, lambda e, k=k, y_v=y_v: e.dma_start(out=y_v, in_=ytile[k]))
            add("io%d" % k, rs, lambda e, k=k: interleave(e, "o%d" % k, ytile[k], 0, N, 2))
            add("io%dL" % k, rs, lambda e, k=k: interleave(e, "o%d" % k, ytile[k], 0, 256, 2))
            add("io%dR" % k, rs, lambda e, k=k: interleave(e, "o%d" % k, ytile[k], 256, N, 2))
            add("qo%d" % k, ["io%d" % k], lambda e, k=k: quantize_y(k))
            add("qo%dL" % k, ["io%dL" % k], lambda e, k=k: quantize_y(k, 0, 256))
            add("qo%dR" % k, ["io%dR" % k], lambda e, k=k: quantize_y(k, 256, N))
            qs = [n for n in ("qo%d" % k, "qo%dL" % k, "qo%dR" % k) if n in queued]
            add("Sc%d" % k, qs, lambda e, k=k, G=G, s=s: e.dma_start(
                out=out_1[G][:, cols(s), :].rearrange("p m t -> p (m t)").bitcast(I32), in_=ycodes[k].bitcast(I32)))
        for G in range(4):
            ks = [k for k in range(8) if UNITS[k][0] == G]
            add("SY%d" % G, ["r%d%d" % (k, t) for k in ks for t in range(4)], lambda e, G=G: e.dma_start(
                out=out_0[cols(G), :].rearrange("(p t) m -> p t m", t=4), in_=ytile["G", G][:]))
            add("SC%d" % G, ["qo%d" % k for k in ks], lambda e, G=G: e.dma_start(
                out=out_1[G].rearrange("p m t -> p (m t)").bitcast(I32), in_=ycodes["G", G][:].bitcast(I32)))
        all_q = [n for n in queued if n.startswith("qo")]
        for q in range(4):
            add("Ss%d" % q, all_q, lambda e, q=q: e.dma_start(
                out=out_2[:, 4 * q:4 * q + 4, :].bitcast(I32), in_=y_scales[32 * q:32 * q + 16, :].bitcast(I32)))

            for s in range(2):
                add("Ss%d%d" % (q, s), [n for n in all_q if UNITS[int(n[2])][1] == s], lambda e, q=q, s=s: e.dma_start(
                    out=out_2[:, 4 * q:4 * q + 4, cols(s)].bitcast(I32), in_=y_scales[32 * q:32 * q + 16, cols(s)].bitcast(I32)))

        queues = [(nc.sync, Q_SYNC), (nc.scalar, Q_ACT), (nc.vector, Q_DVE), (nc.gpsimd, Q_POOL), (nc.tensor, Q_PE)]
        pos = [0] * len(queues)
        done = set()
        ctx.enter_context(tc.manual_schedule())
        while any(pos[i] < len(queues[i][1]) for i in range(len(queues))):
            moved = False
            for i in range(len(queues)):
                e, names = queues[i]
                if pos[i] < len(names) and all(d in done for d in steps[names[pos[i]]][0]):
                    steps[names[pos[i]]][1](e)
                    done.add(names[pos[i]])
                    pos[i] += 1
                    moved = True
            assert moved
